import numpy as np
import ml_dtypes


def mxq(x, axis, fmt="e4m3"):
    dtype, down = {"e4m3": (ml_dtypes.float8_e4m3fn, 7), "e5m2": (ml_dtypes.float8_e5m2, 14)}[fmt]
    v = np.moveaxis(np.asarray(x, np.float32).astype(ml_dtypes.bfloat16).astype(np.float64), axis, -1)
    blocks = v.reshape(v.shape[:-1] + (-1, 32))
    amax = np.abs(blocks).max(-1, keepdims=True)
    byte = np.maximum(np.where(amax > 0, np.frexp(amax)[1] - 1 + 127, 0) - down, 1)
    scale = np.exp2(byte - 127.0)
    codes = (blocks / scale).astype(np.float32).astype(dtype).astype(np.float64)
    return np.moveaxis((codes * scale).reshape(v.shape), -1, axis)


WIDE = False


def mx_kscale(k):
    if not WIDE:
        return np.ones(k)
    levels = np.array([10, -10, 5, -5, 0])
    if k % 512:
        return np.exp2(np.random.permutation(np.resize(levels, k // 32))).repeat(32)
    a = np.empty((k // 512, 16))
    for p in range(k // 512):
        a[p, :8] = np.random.permutation(np.resize(levels, 8))
        for g in range(8):
            far = levels[np.abs(levels - a[p, g]) >= 10]
            a[p, g + 8] = far[np.random.randint(len(far))]
    return np.exp2(a.ravel()).repeat(32)


BF16 = ml_dtypes.bfloat16


def bf(x):
    return np.asarray(x, np.float32).astype(BF16)


def f64(x):
    return np.asarray(x).astype(np.float64)


E2M1 = np.array([0.0, 0.5, 1.0, 1.5, 2.0, 3.0, 4.0, 6.0, -0.0, -0.5, -1.0, -1.5, -2.0, -3.0, -4.0, -6.0])


def pack_weight(w, fmt):
    k, n = w.shape
    w = f64(bf(w)).reshape(k // 32, 32, n)
    amax = np.abs(w).max(1)
    if fmt == "e4m3":
        byte = np.frexp(amax)[1] - 1 + 127 - 7
    else:
        mant, ex = np.frexp(amax / 6.0)
        byte = np.where(mant > 0.5, ex, ex - 1) + 127
    byte = np.clip(np.where(amax > 0, byte, 1), 1, 254)
    scaled = (w * np.exp2(127.0 - byte)[:, None, :]).reshape(k, n).astype(np.float32)
    by_word = np.ascontiguousarray(scaled.reshape(k // 512, 128, 4, n).transpose(0, 1, 3, 2))
    if fmt == "e4m3":
        words = by_word.astype(ml_dtypes.float8_e4m3fn).view(np.uint8)
    else:
        c = by_word.astype(ml_dtypes.float4_e2m1fn).view(np.uint8) & 0xF
        words = c[..., 0::2] | (c[..., 1::2] << 4)
    return np.ascontiguousarray(words), np.ascontiguousarray(byte.astype(np.uint8).reshape(k // 512, 16, n))


def unpack_weight(words, scales, fmt):
    g, p, n, _ = words.shape
    if fmt == "e4m3":
        vals = np.ascontiguousarray(words).view(ml_dtypes.float8_e4m3fn).astype(np.float64)
    else:
        nib = np.empty((g, p, n, 4), np.uint8)
        nib[..., 0::2] = words & 0xF
        nib[..., 1::2] = words >> 4
        vals = E2M1[nib]
    vals = vals * np.repeat(np.exp2(scales.astype(np.float64) - 127.0), 8, axis=1)[..., None]
    return vals.transpose(0, 1, 3, 2).reshape(g * 512, n)
def pack4(w):
    words, scales = pack_weight(w, "e2m1")
    return words.reshape(words.shape[0], 128, -1), scales


def unpack4(words, scales):
    return unpack_weight(words.reshape(words.shape[0], 128, -1, 2), scales, "e2m1")


def planes(Y):
    n, m = Y.shape
    b = f64(bf(Y)).reshape(n // 32, 32, m)
    amax = np.abs(b).max(1)
    byte = np.clip(np.where(amax > 0, np.frexp(amax)[1] - 1 + 127 - 7, 1), 1, 254)
    codes = (b * np.exp2(127.0 - byte)[:, None, :]).reshape(n, m).astype(np.float32).astype(ml_dtypes.float8_e4m3fn).view(np.uint8)
    words = codes.reshape(n // 512, 128, 4, m).transpose(0, 1, 3, 2)
    return np.ascontiguousarray(words), np.ascontiguousarray(byte.astype(np.uint8).reshape(n // 512, 16, m))


T, D, DS, F = 1024, 1024, 1024, 1024


def sigmoid(v):
    return 1.0 / (1.0 + np.exp(-v))


def setup_inputs():
    s, r, t = mx_kscale(D), mx_kscale(DS), mx_kscale(F)
    k_recv = bf(np.random.standard_normal((T, D)) * s)
    k_share = bf(np.random.standard_normal((T, DS)) * r)
    w_recv_words, w_recv_scales = pack4(np.random.standard_normal((D, F)) / np.sqrt(D) / s[:, None])
    w_share_words, w_share_scales = pack4(np.random.standard_normal((DS, F)) / np.sqrt(DS) / r[:, None])
    g_hid = bf((1.0 + 0.1 * np.random.standard_normal(F)) * t)
    w_delta_words, w_delta_scales = pack4(np.random.standard_normal((F, D)) * 2.0 / np.sqrt(F) / t[:, None] * s)
    w_gate_words, w_gate_scales = pack4(np.random.standard_normal((F, D)) * 1.5 / np.sqrt(F) / t[:, None])
    return {
        "k_recv": k_recv,
        "k_share": k_share,
        "w_recv_words": w_recv_words,
        "w_recv_scales": w_recv_scales,
        "w_share_words": w_share_words,
        "w_share_scales": w_share_scales,
        "g_hid": g_hid,
        "w_delta_words": w_delta_words,
        "w_delta_scales": w_delta_scales,
        "w_gate_words": w_gate_words,
        "w_gate_scales": w_gate_scales,
    }


def core(k_recv, k_share, w_recv_words, w_recv_scales, w_share_words, w_share_scales, g_hid, w_delta_words, w_delta_scales, w_gate_words, w_gate_scales):
    kr = f64(k_recv)
    u = (mxq(kr, 1, "e4m3") @ unpack4(w_recv_words, w_recv_scales)) + (mxq(f64(k_share), 1, "e4m3") @ unpack4(w_share_words, w_share_scales))
    h = u * sigmoid(u) * f64(g_hid)[None, :]
    hq = mxq(h, 1, "e4m3")
    delta = hq @ unpack4(w_delta_words, w_delta_scales)
    gate = sigmoid(hq @ unpack4(w_gate_words, w_gate_scales))
    return kr + gate * delta


def reference(k_recv, k_share, w_recv_words, w_recv_scales, w_share_words, w_share_scales, g_hid, w_delta_words, w_delta_scales, w_gate_words, w_gate_scales):
    R_out = core(k_recv, k_share, w_recv_words, w_recv_scales, w_share_words, w_share_scales, g_hid, w_delta_words, w_delta_scales, w_gate_words, w_gate_scales)
    words, scales = planes(R_out)
    return R_out, words, scales

@@ -1,0 +1,295 @@
+from contextlib import ExitStack
+
+import concourse.mybir as mybir
+from concourse.masks import make_identity
+
+F32 = mybir.dt.float32
+BF16 = mybir.dt.bfloat16
+U32 = mybir.dt.uint32
+I32 = mybir.dt.int32
+U8 = mybir.dt.uint8
+E4M3 = mybir.dt.float8_e4m3fn_x4
+E2M1 = mybir.dt.float4_e2m1fn_x4
+ACT = mybir.ActivationFunctionType
+ALU = mybir.AluOpType
+
+P = 128
+T = D = F = 1024
+FLOPS = 4 * 2 * T * D * F
+
+
+def tile_cachetocachegatedkeyfuser_x2_kernel(
+    tc, k_recv, k_share, w_recv_words, w_recv_scales, w_share_words, w_share_scales,
+    g_hid, w_delta_words, w_delta_scales, w_gate_words, w_gate_scales, out_0, out_1, out_2,
+):
+    nc = tc.nc
+    with ExitStack() as ctx:
+        keep = ctx.enter_context(tc.tile_pool(name="keep", bufs=1))
+        work = ctx.enter_context(tc.tile_pool(name="work", bufs=3))
+        psum = ctx.enter_context(tc.psum_pool(name="psum", bufs=8))
+
+
+        warm = keep.tile([P, 1], F32, name="warm")
+        nc.vector.memset(warm[:], 0.0)
+        nc.scalar.activation(out=warm[:], in_=warm[:], func=ACT.Silu)
+
+        def plane(name):
+            return (keep.tile([P, 2, 2048], U8, name=name + "_w", align_bytes=256),
+                    keep.tile([P, 2, 1024], U8, name=name + "_s", align_bytes=256))
+
+        w_raw, s_raw = zip(plane("recv"), plane("share"))
+        wd, sd = plane("delta")
+        wg, sg = plane("gate")
+        for s in (s_raw[0], s_raw[1], sd, sg):
+            nc.vector.memset(s[:].rearrange("p g n -> p (g n)").bitcast(I32), 0)
+        ident = keep.tile([P, P], F32, name="ident")
+        make_identity(nc, ident[:])
+
+        k_raw = [[keep.tile([P, 4, 1024], BF16, name="k%d%d" % (x, g), align_bytes=256) for g in range(2)] for x in range(2)]
+        k_hbm = [k.rearrange("(g p t) d -> g p t d", g=2, t=4) for k in (k_recv, k_share)]
+
+        def load_words(tile, hbm, gf=None):
+            b = slice(0, 2048) if gf is None else slice(1024 * gf, 1024 * (gf + 1))
+            nc.sync.dma_start(out=tile[:, :, b].bitcast(I32), in_=hbm[:, :, b].rearrange("g p n -> p g n").bitcast(I32))
+
+        def load_scales(tile, hbm):
+            for q in range(4):
+                nc.sync.dma_start(
+                    out=tile[32 * q : 32 * q + 4, :, :].bitcast(I32),
+                    in_=hbm[:, 4 * q : 4 * q + 4, :].rearrange("g r n -> r g n").bitcast(I32),
+                )
+
+        def load_x(x, g, t0, t1):
+            nc.sync.dma_start(out=k_raw[x][g][:, t0:t1, :], in_=k_hbm[x][g, :, t0:t1, :])
+
+        load_x(0, 0, 0, 1)
+        load_x(0, 0, 1, 2)
+        load_x(0, 0, 2, 4)
+        load_words(w_raw[0], w_recv_words, 0)
+        load_scales(s_raw[0], w_recv_scales)
+        load_x(1, 0, 0, 2)
+        load_x(1, 0, 2, 4)
+        load_words(w_raw[1], w_share_words, 0)
+        load_scales(s_raw[1], w_share_scales)
+        load_words(w_raw[0], w_recv_words, 1)
+        load_words(w_raw[1], w_share_words, 1)
+        gt = keep.tile([P, 2, 4], BF16, name="gt")
+        nc.sync.dma_start(out=gt[:], in_=g_hid.rearrange("(g p t) -> p g t", g=2, t=4))
+        load_x(0, 1, 0, 4)
+        load_x(1, 1, 0, 4)
+        load_scales(sd, w_delta_scales)
+        load_scales(sg, w_gate_scales)
+        load_words(wd, w_delta_words)
+        load_words(wg, w_gate_words)
+
+        wp = [keep.tile([P, 2, 2, 4, 256], U8, name="wp%d" % x, align_bytes=256) for x in range(2)]
+        sp = [keep.tile([P, 2, 2, 4, 128], U8, name="sp%d" % x, align_bytes=256) for x in range(2)]
+
+        def perm_w(x, gf, c):
+            nc.vector.tensor_copy(
+                out=wp[x][:, c, gf, :, :].rearrange("p t (m b) -> p t m b", b=2),
+                in_=w_raw[x][:, c, 1024 * gf : 1024 * (gf + 1)].rearrange("p (m t b) -> p t m b", t=4, b=2),
+            )
+
+        def perm_s(x, gf):
+            nc.vector.tensor_copy(
+                out=sp[x][:, :, gf, :, :],
+                in_=s_raw[x][:, :, 512 * gf : 512 * (gf + 1)].rearrange("p c (m t) -> p c t m", t=4),
+            )
+
+        xc = {}
+        xs = {}
+        grp = {}
+        for x in range(2):
+            for g in range(2):
+                for c in range(2):
+                    xc[x, g, c] = keep.tile([P, 512], U32, name="xc%d%d%d" % (x, g, c), align_bytes=256)
+                    xs[x, g, c] = keep.tile([P, 512], U8, name="xs%d%d%d" % (x, g, c), align_bytes=256)
+
+        def bank():
+            return psum.tile([P, 512], F32, name="ps")
+
+        def transposes(x, g, tp):
+            for c in range(2):
+                if tp == 0:
+                    grp[x, g, c] = work.tile([P, 512, 4], BF16, name="grp%d" % c, align_bytes=256, bufs=2)
+                xt = bank()
+                xt4 = xt[:].rearrange("p (a u r) -> p a u r", a=2, u=2)
+                for tt in range(2):
+                    words = k_raw[x][g][:, 2 * tp + tt, :].bitcast(F32)
+                    for u in range(2):
+                        nc.tensor.transpose(xt4[:, tt, u, :], words[:, 256 * c + u : 256 * (c + 1) : 2], ident[:])
+                dst = grp[x, g, c][:, 256 * tp : 256 * (tp + 1), :].bitcast(F32).rearrange("p (a r) u -> p a r u", a=2)
+                nc.scalar.copy(out=dst, in_=xt4.rearrange("p a u r -> p a r u"))
+
+        def quantize_x(x, g, c, tp):
+            n = slice(256 * tp, 256 * (tp + 1))
+            nc.vector.quantize_mx(out=xc[x, g, c][:, n].bitcast(E4M3), scales=xs[x, g, c][:, n],
+                                  in_=grp[x, g, c][:, n, :].rearrange("p n t -> p (n t)"))
+
+        def quantize_both(x, g, tp):
+            quantize_x(x, g, 0, tp)
+            quantize_x(x, g, 1, tp)
+
+        def s1_pass(b, x, g, gf, t, c):
+            nc.tensor.matmul_mx(
+                out=b[:],
+                lhsT=wp[x][:, c, gf, t, :].bitcast(E2M1), lhsT_scale=sp[x][:, c, gf, t, :],
+                rhs=xc[x, g, c][:].bitcast(E4M3), rhs_scale=xs[x, g, c][:],
+                start=(x == 0 and c == 0), stop=(x == 1 and c == 1),
+            )
+
+        hq = {}
+        hs = {}
+        h32 = {}
+        ht = {}
+        SPLIT = ()
+
+        def silu(g, gf, t, b):
+            if t == 0:
+                h32[g, gf] = work.tile([P, 4, 512], F32, name="h32", bufs=2)
+                if (g, gf) in SPLIT:
+                    ht[g, gf] = work.tile([P, 4, 512], BF16, name="ht", align_bytes=256, bufs=2)
+            nc.scalar.activation(out=h32[g, gf][:, t, :], in_=b[:], func=ACT.Silu)
+            if (g, gf) in SPLIT:
+                nc.vector.tensor_scalar(out=ht[g, gf][:, t, :], in0=h32[g, gf][:, t, :], scalar1=gt[:, gf, t : t + 1],
+                                        scalar2=None, op0=ALU.mult)
+
+        def hidden(g, gf):
+            hb = work.tile([P, 512, 4], BF16, name="hb", align_bytes=256, bufs=2)
+            hq[g, gf] = keep.tile([P, 512], U32, name="hc%d%d" % (g, gf), align_bytes=256)
+            hs[g, gf] = keep.tile([P, 512], U8, name="hs%d%d" % (g, gf), align_bytes=256)
+            for k in range(4):
+                n = slice(128 * k, 128 * (k + 1))
+                if (g, gf) in SPLIT:
+                    nc.scalar.copy(out=hb[:, n, :], in_=ht[g, gf][:, :, n].rearrange("p t n -> p n t"))
+                else:
+                    nc.vector.tensor_tensor(
+                        out=hb[:, n, :], in0=h32[g, gf][:, :, n].rearrange("p t n -> p n t"),
+                        in1=gt[:, gf, :].unsqueeze(1).to_broadcast([P, 128, 4]), op=ALU.mult)
+                nc.vector.quantize_mx(out=hq[g, gf][:, n].bitcast(E4M3), scales=hs[g, gf][:, n],
+                                      in_=hb[:, n, :].rearrange("p n t -> p (n t)"))
+
+        o0 = out_0.rearrange("(g p t) d -> g p t d", g=2, t=4)
+
+        def s2_bank(g, t, nh, w, s):
+            b = bank()
+            for gf in range(2):
+                nc.tensor.matmul_mx(
+                    out=b[:],
+                    lhsT=hq[g, gf][:, 128 * t : 128 * (t + 1)].bitcast(E4M3),
+                    lhsT_scale=hs[g, gf][:, 128 * t : 128 * (t + 1)],
+                    rhs=w[:, gf, 1024 * nh : 1024 * (nh + 1)].bitcast(E2M1),
+                    rhs_scale=s[:, gf, 512 * nh : 512 * (nh + 1)],
+                    start=(gf == 0), stop=(gf == 1),
+                )
+            return b
+
+        r = {}
+
+        def s2_unit(i):
+            g, nh, t = i // 8, (i // 4) % 2, i % 4
+            cols = slice(512 * nh, 512 * (nh + 1))
+            if t == 0:
+                r[g, nh] = work.tile([P, 4, 512], F32, name="r", bufs=3)
+            gate = s2_bank(g, t, nh, wg, sg)
+            delta = s2_bank(g, t, nh, wd, sd)
+            th = work.tile([P, 512], F32, name="th", bufs=4)
+            nc.scalar.activation(out=th[:], in_=gate[:], func=ACT.Tanh, scale=0.5)
+            prod = work.tile([P, 512], F32, name="prod", bufs=4)
+            nc.vector.scalar_tensor_tensor(out=prod[:], in0=th[:], scalar=1.0, in1=delta[:], op0=ALU.add, op1=ALU.mult)
+            nc.vector.scalar_tensor_tensor(out=r[g, nh][:, t, :], in0=prod[:], scalar=0.5,
+                                           in1=k_raw[0][g][:, t, cols], op0=ALU.mult, op1=ALU.add)
+            nc.sync.dma_start(out=o0[g, :, t, cols], in_=r[g, nh][:, t, :])
+            if t == 3:
+                planes(g, nh, i == 15)
+
+        def planes(g, nh, last):
+            cols = slice(512 * nh, 512 * (nh + 1))
+            rb = work.tile([P, 512, 4], BF16, name="rb", align_bytes=256, bufs=2)
+            codes = work.tile([P, 512], U32, name="oc", align_bytes=256, bufs=2)
+            scl = work.tile([P, 512], U8, name="os", align_bytes=256, bufs=2)
+            for k in range(4):
+                m = slice(128 * k, 128 * (k + 1))
+                src = r[g, nh][:, :, m].rearrange("p t m -> p m t")
+                if last and k % 2 == 1:
+                    nc.vector.tensor_copy(out=rb[:, m, :], in_=src)
+                else:
+                    nc.scalar.copy(out=rb[:, m, :], in_=src)
+                if k % 2 == 1:
+                    m = slice(128 * (k - 1), 128 * (k + 1))
+                    nc.vector.quantize_mx(out=codes[:, m].bitcast(E4M3), scales=scl[:, m],
+                                          in_=rb[:, m, :].rearrange("p m t -> p (m t)"))
+            nc.sync.dma_start(
+                out=out_1[g, :, cols, :].rearrange("p m t -> p (m t)").bitcast(I32), in_=codes[:].bitcast(I32))
+            for q in range(4):
+                nc.sync.dma_start(out=out_2[g, 4 * q : 4 * q + 4, cols].bitcast(I32),
+                                  in_=scl[32 * q : 32 * q + 4, :].bitcast(I32))
+
+        for tp in range(2):
+            transposes(0, 0, tp)
+        transposes(1, 0, 0)
+        quantize_both(0, 0, 0)
+        perm_w(0, 0, 0)
+        perm_s(0, 0)
+        perm_w(0, 0, 1)
+        quantize_both(0, 0, 1)
+        b0 = [bank() for t in range(4)]
+        for c in range(2):
+            for t in range(4):
+                s1_pass(b0[t], 0, 0, 0, t, c)
+        transposes(1, 0, 1)
+        perm_w(1, 0, 0)
+        perm_w(1, 0, 1)
+        perm_s(1, 0)
+        quantize_both(1, 0, 0)
+        quantize_both(1, 0, 1)
+        perm_w(0, 1, 0)
+        perm_w(0, 1, 1)
+        perm_s(0, 1)
+        perm_w(1, 1, 0)
+        perm_w(1, 1, 1)
+        perm_s(1, 1)
+        b1 = []
+        for t in range(3):
+            b1.append(bank())
+            for c in range(2):
+                s1_pass(b1[t], 0, 0, 1, t, c)
+        for t in range(4):
+            for c in range(2):
+                s1_pass(b0[t], 1, 0, 0, t, c)
+            silu(0, 0, t, b0[t])
+        hidden(0, 0)
+        for t in range(4):
+            if t == 3:
+                b1.append(bank())
+                for c in range(2):
+                    s1_pass(b1[t], 0, 0, 1, t, c)
+            for c in range(2):
+                s1_pass(b1[t], 1, 0, 1, t, c)
+            silu(0, 1, t, b1[t])
+            if t == 1:
+                transposes(0, 1, 0)
+                quantize_both(0, 1, 0)
+        transposes(0, 1, 1)
+        quantize_both(0, 1, 1)
+        hidden(0, 1)
+        for tp in range(2):
+            transposes(1, 1, tp)
+            quantize_both(1, 1, tp)
+
+        def s1_unit(j):
+            gf, t = divmod(j, 4)
+            b = bank()
+            for x in range(2):
+                for c in range(2):
+                    s1_pass(b, x, 1, gf, t, c)
+            silu(1, gf, t, b)
+            if t == 3:
+                hidden(1, gf)
+
+        for u in (0, 1, 8, 9, 2, 10, 11, 3, 12, 13, 4, 14, 5, 15, 6, 7, 16, 17, 18, 19, 20, 21, 22, 23):
+            if u < 8:
+                s1_unit(u)
+            else:
+                s2_unit(u - 8)

@@ -27,6 +27,7 @@ def tile_cachetocachegatedkeyfuser_x2_kernel(
         keep = ctx.enter_context(tc.tile_pool(name="keep", bufs=1))
         work = ctx.enter_context(tc.tile_pool(name="work", bufs=3))
         psum = ctx.enter_context(tc.psum_pool(name="psum", bufs=8))
+        ctx.enter_context(tc.manual_schedule())
 
 
         warm = keep.tile([P, 1], F32, name="warm")
@@ -109,18 +110,44 @@ def tile_cachetocachegatedkeyfuser_x2_kernel(
         def bank():
             return psum.tile([P, 512], F32, name="ps")
 
+        k_words = {}
+        DEINT = ((0, 1), (1, 1))
+
+        def deinterleave(x, g, tp):
+            if tp == 0:
+                k_words[x, g] = keep.tile([P, 4, 2, 2, 128], F32, name="kw%d%d" % (x, g), align_bytes=256)
+            t = slice(2 * tp, 2 * tp + 2)
+            nc.vector.tensor_copy(out=k_words[x, g][:, t].rearrange("p t c u w -> p (t c) u w"),
+                           in_=k_raw[x][g][:, t, :].bitcast(F32).rearrange("p t (c w u) -> p (t c) u w", c=2, u=2))
+
         def transposes(x, g, tp):
             for c in range(2):
                 if tp == 0:
-                    grp[x, g, c] = work.tile([P, 512, 4], BF16, name="grp%d" % c, align_bytes=256, bufs=2)
+                    grp[x, g, c] = work.tile([P, 512, 4], BF16, name="grp%d" % c, align_bytes=256, bufs=3)
                 xt = bank()
                 xt4 = xt[:].rearrange("p (a u r) -> p a u r", a=2, u=2)
                 for tt in range(2):
-                    words = k_raw[x][g][:, 2 * tp + tt, :].bitcast(F32)
                     for u in range(2):
-                        nc.tensor.transpose(xt4[:, tt, u, :], words[:, 256 * c + u : 256 * (c + 1) : 2], ident[:])
-                dst = grp[x, g, c][:, 256 * tp : 256 * (tp + 1), :].bitcast(F32).rearrange("p (a r) u -> p a r u", a=2)
-                nc.scalar.copy(out=dst, in_=xt4.rearrange("p a u r -> p a r u"))
+                        if (x, g) in DEINT:
+                            words = k_words[x, g][:, 2 * tp + tt, c, u, :]
+                        else:
+                            words = k_raw[x][g][:, 2 * tp + tt, :].bitcast(F32)[:, 256 * c + u : 256 * (c + 1) : 2]
+                        nc.tensor.transpose(xt4[:, tt, u, :], words, ident[:])
+                copy_q.append((copy_out, (x, g, c, tp, xt4)))
+
+        def copy_out(x, g, c, tp, xt4):
+            dst = grp[x, g, c][:, 256 * tp : 256 * (tp + 1), :].bitcast(F32).rearrange("p (a r) u -> p a r u", a=2)
+            nc.scalar.copy(out=dst, in_=xt4.rearrange("p a u r -> p a r u"))
+
+        copy_q = []
+        act_q = []
+        dve_q = []
+
+        def run(q, n=99):
+            for i in range(n):
+                if q:
+                    f, a = q.pop(0)
+                    f(*a)
 
         def quantize_x(x, g, c, tp):
             n = slice(256 * tp, 256 * (tp + 1))
@@ -143,32 +170,54 @@ def tile_cachetocachegatedkeyfuser_x2_kernel(
         hs = {}
         h32 = {}
         ht = {}
-        SPLIT = ()
+        SPLIT = ((1, 0), (1, 1))
+
+        hb = {}
 
         def silu(g, gf, t, b):
             if t == 0:
                 h32[g, gf] = work.tile([P, 4, 512], F32, name="h32", bufs=2)
+                hb[g, gf] = work.tile([P, 512, 4], BF16, name="hb", align_bytes=256, bufs=2)
+                hq[g, gf] = keep.tile([P, 512], U32, name="hc%d%d" % (g, gf), align_bytes=256)
+                hs[g, gf] = keep.tile([P, 512], U8, name="hs%d%d" % (g, gf), align_bytes=256)
                 if (g, gf) in SPLIT:
                     ht[g, gf] = work.tile([P, 4, 512], BF16, name="ht", align_bytes=256, bufs=2)
             nc.scalar.activation(out=h32[g, gf][:, t, :], in_=b[:], func=ACT.Silu)
-            if (g, gf) in SPLIT:
-                nc.vector.tensor_scalar(out=ht[g, gf][:, t, :], in0=h32[g, gf][:, t, :], scalar1=gt[:, gf, t : t + 1],
-                                        scalar2=None, op0=ALU.mult)
+
+        def gain(g, gf, t):
+            nc.vector.tensor_scalar(out=ht[g, gf][:, t, :], in0=h32[g, gf][:, t, :], scalar1=gt[:, gf, t : t + 1],
+                                    scalar2=None, op0=ALU.mult)
+
+        def weave(g, gf, k):
+            c = slice(32 * k, 32 * (k + 1))
+            nc.scalar.copy(out=hb[g, gf][:].rearrange("p (c i) t -> p c t i", i=4)[:, c],
+                           in_=ht[g, gf][:].rearrange("p t (c i) -> p c t i", i=4)[:, c])
+
+        woven = []
+
+        def weave_q(g, gf, k):
+            weave(g, gf, k)
+            woven.append((g, gf, k))
+            dve_q.append((hidden_q, (g, gf, k)))
+
+        def hidden_tt(g, gf, k):
+            c = slice(32 * k, 32 * (k + 1))
+            nc.vector.tensor_tensor(
+                out=hb[g, gf][:].rearrange("p (c i) t -> p c t i", i=4)[:, c],
+                in0=h32[g, gf][:].rearrange("p t (c i) -> p c t i", i=4)[:, c],
+                in1=gt[:, gf, :].unsqueeze(1).unsqueeze(3).to_broadcast([P, 32, 4, 4]), op=ALU.mult)
+
+        def hidden_q(g, gf, k):
+            n = slice(128 * k, 128 * (k + 1))
+            nc.vector.quantize_mx(out=hq[g, gf][:, n].bitcast(E4M3), scales=hs[g, gf][:, n],
+                                  in_=hb[g, gf][:, n, :].rearrange("p n t -> p (n t)"))
 
         def hidden(g, gf):
-            hb = work.tile([P, 512, 4], BF16, name="hb", align_bytes=256, bufs=2)
-            hq[g, gf] = keep.tile([P, 512], U32, name="hc%d%d" % (g, gf), align_bytes=256)
-            hs[g, gf] = keep.tile([P, 512], U8, name="hs%d%d" % (g, gf), align_bytes=256)
-            for k in range(4):
-                n = slice(128 * k, 128 * (k + 1))
-                if (g, gf) in SPLIT:
-                    nc.scalar.copy(out=hb[:, n, :], in_=ht[g, gf][:, :, n].rearrange("p t n -> p n t"))
-                else:
-                    nc.vector.tensor_tensor(
-                        out=hb[:, n, :], in0=h32[g, gf][:, :, n].rearrange("p t n -> p n t"),
-                        in1=gt[:, gf, :].unsqueeze(1).to_broadcast([P, 128, 4]), op=ALU.mult)
-                nc.vector.quantize_mx(out=hq[g, gf][:, n].bitcast(E4M3), scales=hs[g, gf][:, n],
-                                      in_=hb[:, n, :].rearrange("p n t -> p (n t)"))
+            hidden_tt(g, gf, 0)
+            for k in range(1, 4):
+                hidden_tt(g, gf, k)
+                hidden_q(g, gf, k - 1)
+            hidden_q(g, gf, 3)
 
         o0 = out_0.rearrange("(g p t) d -> g p t d", g=2, t=4)
 
@@ -187,109 +236,143 @@ def tile_cachetocachegatedkeyfuser_x2_kernel(
 
         r = {}
 
-        def s2_unit(i):
-            g, nh, t = i // 8, (i // 4) % 2, i % 4
+        adds = []
+        late = []
+        ready = []
+
+        def s2_add(g, nh, t, prod):
             cols = slice(512 * nh, 512 * (nh + 1))
-            if t == 0:
-                r[g, nh] = work.tile([P, 4, 512], F32, name="r", bufs=3)
-            gate = s2_bank(g, t, nh, wg, sg)
-            delta = s2_bank(g, t, nh, wd, sd)
-            th = work.tile([P, 512], F32, name="th", bufs=4)
-            nc.scalar.activation(out=th[:], in_=gate[:], func=ACT.Tanh, scale=0.5)
-            prod = work.tile([P, 512], F32, name="prod", bufs=4)
-            nc.vector.scalar_tensor_tensor(out=prod[:], in0=th[:], scalar=1.0, in1=delta[:], op0=ALU.add, op1=ALU.mult)
             nc.vector.scalar_tensor_tensor(out=r[g, nh][:, t, :], in0=prod[:], scalar=0.5,
                                            in1=k_raw[0][g][:, t, cols], op0=ALU.mult, op1=ALU.add)
             nc.sync.dma_start(out=o0[g, :, t, cols], in_=r[g, nh][:, t, :])
             if t == 3:
-                planes(g, nh, i == 15)
+                late.append((g, nh))
 
-        def planes(g, nh, last):
-            cols = slice(512 * nh, 512 * (nh + 1))
-            rb = work.tile([P, 512, 4], BF16, name="rb", align_bytes=256, bufs=2)
-            codes = work.tile([P, 512], U32, name="oc", align_bytes=256, bufs=2)
-            scl = work.tile([P, 512], U8, name="os", align_bytes=256, bufs=2)
-            for k in range(4):
-                m = slice(128 * k, 128 * (k + 1))
-                src = r[g, nh][:, :, m].rearrange("p t m -> p m t")
-                if last and k % 2 == 1:
-                    nc.vector.tensor_copy(out=rb[:, m, :], in_=src)
-                else:
-                    nc.scalar.copy(out=rb[:, m, :], in_=src)
-                if k % 2 == 1:
-                    m = slice(128 * (k - 1), 128 * (k + 1))
-                    nc.vector.quantize_mx(out=codes[:, m].bitcast(E4M3), scales=scl[:, m],
-                                          in_=rb[:, m, :].rearrange("p m t -> p (m t)"))
-            nc.sync.dma_start(
-                out=out_1[g, :, cols, :].rearrange("p m t -> p (m t)").bitcast(I32), in_=codes[:].bitcast(I32))
-            for q in range(4):
-                nc.sync.dma_start(out=out_2[g, 4 * q : 4 * q + 4, cols].bitcast(I32),
-                                  in_=scl[32 * q : 32 * q + 4, :].bitcast(I32))
+        def plane_cvt(g, nh, k):
+            if k == 0:
+                r[g, nh, 0] = (work.tile([P, 512, 4], BF16, name="rb", align_bytes=256, bufs=2),
+                               work.tile([P, 512], U32, name="oc", align_bytes=256, bufs=2),
+                               work.tile([P, 512], U8, name="os", align_bytes=256, bufs=2))
+            rb = r[g, nh, 0][0]
+            c = slice(32 * k, 32 * (k + 1))
+            dst = rb[:].rearrange("p (c i) t -> p c t i", i=4)[:, c]
+            src = r[g, nh][:].rearrange("p t (c i) -> p c t i", i=4)[:, c]
+            if (g, nh, k) in DVE_LAST:
+                nc.vector.tensor_copy(out=dst, in_=src)
+            else:
+                nc.scalar.copy(out=dst, in_=src)
+            if k % 2 == 1:
+                dve_q.append((plane_q, (g, nh, k // 2)))
 
-        for tp in range(2):
-            transposes(0, 0, tp)
-        transposes(1, 0, 0)
+        DVE_LAST = ((1, 1, 1), (1, 1, 3))
+
+        def plane_q(g, nh, k):
+            rb, codes, scl = r[g, nh, 0]
+            m = slice(256 * k, 256 * (k + 1))
+            nc.vector.quantize_mx(out=codes[:, m].bitcast(E4M3), scales=scl[:, m],
+                                  in_=rb[:, m, :].rearrange("p m t -> p (m t)"))
+            if k == 1:
+                cols = slice(512 * nh, 512 * (nh + 1))
+                nc.sync.dma_start(
+                    out=out_1[g, :, cols, :].rearrange("p m t -> p (m t)").bitcast(I32), in_=codes[:].bitcast(I32))
+                for q in range(4):
+                    nc.sync.dma_start(out=out_2[g, 4 * q : 4 * q + 4, cols].bitcast(I32),
+                                      in_=scl[32 * q : 32 * q + 4, :].bitcast(I32))
+
+        for x in range(2):
+            for tp in range(2):
+                transposes(x, 0, tp)
+                run(copy_q)
         quantize_both(0, 0, 0)
         perm_w(0, 0, 0)
-        perm_s(0, 0)
         perm_w(0, 0, 1)
+        perm_s(0, 0)
         quantize_both(0, 0, 1)
         b0 = [bank() for t in range(4)]
         for c in range(2):
             for t in range(4):
                 s1_pass(b0[t], 0, 0, 0, t, c)
-        transposes(1, 0, 1)
+        quantize_both(1, 0, 0)
         perm_w(1, 0, 0)
         perm_w(1, 0, 1)
         perm_s(1, 0)
-        quantize_both(1, 0, 0)
         quantize_both(1, 0, 1)
-        perm_w(0, 1, 0)
-        perm_w(0, 1, 1)
-        perm_s(0, 1)
-        perm_w(1, 1, 0)
-        perm_w(1, 1, 1)
-        perm_s(1, 1)
-        b1 = []
-        for t in range(3):
-            b1.append(bank())
-            for c in range(2):
-                s1_pass(b1[t], 0, 0, 1, t, c)
+        for x in range(2):
+            perm_w(x, 1, 0)
+            perm_w(x, 1, 1)
+            perm_s(x, 1)
         for t in range(4):
             for c in range(2):
                 s1_pass(b0[t], 1, 0, 0, t, c)
             silu(0, 0, t, b0[t])
+        for x in range(2):
+            if (x, 1) in DEINT:
+                deinterleave(x, 1, 0)
+                deinterleave(x, 1, 1)
         hidden(0, 0)
         for t in range(4):
-            if t == 3:
-                b1.append(bank())
-                for c in range(2):
-                    s1_pass(b1[t], 0, 0, 1, t, c)
-            for c in range(2):
-                s1_pass(b1[t], 1, 0, 1, t, c)
-            silu(0, 1, t, b1[t])
-            if t == 1:
-                transposes(0, 1, 0)
-                quantize_both(0, 1, 0)
-        transposes(0, 1, 1)
-        quantize_both(0, 1, 1)
-        hidden(0, 1)
-        for tp in range(2):
-            transposes(1, 1, tp)
-            quantize_both(1, 1, tp)
-
-        def s1_unit(j):
-            gf, t = divmod(j, 4)
-            b = bank()
+            b1 = bank()
             for x in range(2):
                 for c in range(2):
-                    s1_pass(b, x, 1, gf, t, c)
-            silu(1, gf, t, b)
-            if t == 3:
-                hidden(1, gf)
+                    s1_pass(b1, x, 0, 1, t, c)
+            silu(0, 1, t, b1)
+            if t == 1:
+                for x in range(2):
+                    for tp in range(2):
+                        transposes(x, 1, tp)
+                        run(copy_q)
+                        quantize_both(x, 1, tp)
+        hidden(0, 1)
 
-        for u in (0, 1, 8, 9, 2, 10, 11, 3, 12, 13, 4, 14, 5, 15, 6, 7, 16, 17, 18, 19, 20, 21, 22, 23):
+        for u in (0, 1, 8, 9, 2, 10, 3, 11, 4, 12, 5, 13, 6, 7, 14, 15, 16, 17, 18, 19, 20, 21, 22, 23):
             if u < 8:
-                s1_unit(u)
+                gf, t = divmod(u, 4)
+                b = bank()
+                for x in range(2):
+                    for c in range(2):
+                        s1_pass(b, x, 1, gf, t, c)
+                silu(1, gf, t, b)
+                run(dve_q, 2)
+                if (1, gf) in SPLIT:
+                    gain(1, gf, t)
+                    if t == 3:
+                        act_q = [(weave_q, (1, gf, k)) for k in range(4)] + act_q
+                elif t == 3:
+                    hidden(1, gf)
             else:
-                s2_unit(u - 8)
+                g, nh, t = (u - 8) // 8, (u // 4) % 2, u % 4
+                if u == 16:
+                    run(act_q, 2)
+                if u >= 16 and u < 20 and (1, 1) in SPLIT:
+                    while (1, 1, t) not in woven:
+                        run(act_q, 1)
+                    run(dve_q)
+                if t == 0:
+                    r[g, nh] = work.tile([P, 4, 512], F32, name="r", bufs=3)
+                gate = s2_bank(g, t, nh, wg, sg)
+                delta = s2_bank(g, t, nh, wd, sd)
+                th = work.tile([P, 512], F32, name="th", bufs=4)
+                nc.scalar.activation(out=th[:], in_=gate[:], func=ACT.Tanh, scale=0.5)
+                run(dve_q, 2)
+                prod = work.tile([P, 512], F32, name="prod", bufs=4)
+                nc.vector.scalar_tensor_tensor(out=prod[:], in0=th[:], scalar=1.0, in1=delta[:], op0=ALU.add, op1=ALU.mult)
+                adds.append((s2_add, (g, nh, t, prod)))
+                if len(adds) > 1:
+                    run(adds, 1)
+            if copy_q:
+                run(copy_q, 2)
+                if not copy_q:
+                    quantize_both(1, 1, 0)
+                    quantize_both(1, 1, 1)
+            else:
+                run(act_q, 1)
+            if late and late[0] in ready:
+                act_q.extend((plane_cvt, late[0] + (k,)) for k in range(4))
+                late.pop(0)
+            ready[:] = late
+        run(adds)
+        for gn in late:
+            act_q.extend((plane_cvt, gn + (k,)) for k in range(4))
+        while act_q:
+            run(act_q, 1)
+            run(dve_q)

@@ -53,9 +53,9 @@ def tile_cachetocachegatedkeyfuser_x2_kernel(
             b = slice(0, 2048) if gf is None else slice(1024 * gf, 1024 * (gf + 1))
             nc.sync.dma_start(out=tile[:, :, b].bitcast(I32), in_=hbm[:, :, b].rearrange("g p n -> p g n").bitcast(I32))
 
-        def load_scales(tile, hbm):
+        def load_scales(tile, hbm, engine):
             for q in range(4):
-                nc.sync.dma_start(
+                engine.dma_start(
                     out=tile[32 * q : 32 * q + 4, :, :].bitcast(I32),
                     in_=hbm[:, 4 * q : 4 * q + 4, :].rearrange("g r n -> r g n").bitcast(I32),
                 )
@@ -67,19 +67,19 @@ def tile_cachetocachegatedkeyfuser_x2_kernel(
         load_x(0, 0, 1, 2)
         load_x(0, 0, 2, 4)
         load_words(w_raw[0], w_recv_words, 0)
-        load_scales(s_raw[0], w_recv_scales)
+        load_scales(s_raw[0], w_recv_scales, nc.scalar)
         load_x(1, 0, 0, 2)
         load_x(1, 0, 2, 4)
         load_words(w_raw[1], w_share_words, 0)
-        load_scales(s_raw[1], w_share_scales)
+        load_scales(s_raw[1], w_share_scales, nc.sync)
         load_words(w_raw[0], w_recv_words, 1)
         load_words(w_raw[1], w_share_words, 1)
         gt = keep.tile([P, 2, 4], BF16, name="gt")
         nc.sync.dma_start(out=gt[:], in_=g_hid.rearrange("(g p t) -> p g t", g=2, t=4))
         load_x(0, 1, 0, 4)
         load_x(1, 1, 0, 4)
-        load_scales(sd, w_delta_scales)
-        load_scales(sg, w_gate_scales)
+        load_scales(sd, w_delta_scales, nc.sync)
+        load_scales(sg, w_gate_scales, nc.sync)
         load_words(wd, w_delta_words)
         load_words(wg, w_gate_words)
 
@@ -142,6 +142,7 @@ def tile_cachetocachegatedkeyfuser_x2_kernel(
         copy_q = []
         act_q = []
         dve_q = []
+        tt_q = []
 
         def run(q, n=99):
             for i in range(n):
@@ -170,7 +171,7 @@ def tile_cachetocachegatedkeyfuser_x2_kernel(
         hs = {}
         h32 = {}
         ht = {}
-        SPLIT = ((1, 0), (1, 1))
+        SPLIT = ()
 
         hb = {}
 
@@ -237,6 +238,7 @@ def tile_cachetocachegatedkeyfuser_x2_kernel(
         r = {}
 
         adds = []
+        done = {}
         late = []
         ready = []
 
@@ -245,14 +247,18 @@ def tile_cachetocachegatedkeyfuser_x2_kernel(
             nc.vector.scalar_tensor_tensor(out=r[g, nh][:, t, :], in0=prod[:], scalar=0.5,
                                            in1=k_raw[0][g][:, t, cols], op0=ALU.mult, op1=ALU.add)
             nc.sync.dma_start(out=o0[g, :, t, cols], in_=r[g, nh][:, t, :])
-            if t == 3:
+            done[g, nh] += 1
+            if done[g, nh] == 4:
                 late.append((g, nh))
+
+        out_scales = [keep.tile([P, 1024], U8, name="os%d" % g, align_bytes=256) for g in range(2)]
+        stored = [0, 0]
 
         def plane_cvt(g, nh, k):
             if k == 0:
                 r[g, nh, 0] = (work.tile([P, 512, 4], BF16, name="rb", align_bytes=256, bufs=2),
                                work.tile([P, 512], U32, name="oc", align_bytes=256, bufs=2),
-                               work.tile([P, 512], U8, name="os", align_bytes=256, bufs=2))
+                               out_scales[g][:, 512 * nh : 512 * (nh + 1)])
             rb = r[g, nh, 0][0]
             c = slice(32 * k, 32 * (k + 1))
             dst = rb[:].rearrange("p (c i) t -> p c t i", i=4)[:, c]
@@ -264,30 +270,33 @@ def tile_cachetocachegatedkeyfuser_x2_kernel(
             if k % 2 == 1:
                 dve_q.append((plane_q, (g, nh, k // 2)))
 
-        DVE_LAST = ((1, 1, 1), (1, 1, 3))
+        DVE_LAST = ((1, 1, 0), (1, 1, 1), (1, 1, 2), (1, 1, 3))
 
         def plane_q(g, nh, k):
             rb, codes, scl = r[g, nh, 0]
             m = slice(256 * k, 256 * (k + 1))
             nc.vector.quantize_mx(out=codes[:, m].bitcast(E4M3), scales=scl[:, m],
                                   in_=rb[:, m, :].rearrange("p m t -> p (m t)"))
-            if k == 1:
-                cols = slice(512 * nh, 512 * (nh + 1))
-                nc.sync.dma_start(
-                    out=out_1[g, :, cols, :].rearrange("p m t -> p (m t)").bitcast(I32), in_=codes[:].bitcast(I32))
+            c = slice(512 * nh + 256 * k, 512 * nh + 256 * (k + 1))
+            nc.sync.dma_start(out=out_1[g, :, c, :].rearrange("p m t -> p (m t)").bitcast(I32), in_=codes[:, m].bitcast(I32))
+            stored[g] += 1
+            if stored[g] == 4:
                 for q in range(4):
-                    nc.sync.dma_start(out=out_2[g, 4 * q : 4 * q + 4, cols].bitcast(I32),
-                                      in_=scl[32 * q : 32 * q + 4, :].bitcast(I32))
+                    nc.sync.dma_start(out=out_2[g, 4 * q : 4 * q + 4, :].bitcast(I32),
+                                      in_=out_scales[g][32 * q : 32 * q + 4, :].bitcast(I32))
 
-        for x in range(2):
-            for tp in range(2):
-                transposes(x, 0, tp)
-                run(copy_q)
+        for tp in range(2):
+            transposes(0, 0, tp)
+            run(copy_q)
+        transposes(1, 0, 0)
+        run(copy_q)
+        transposes(1, 0, 1)
+        run(copy_q)
         quantize_both(0, 0, 0)
         perm_w(0, 0, 0)
         perm_w(0, 0, 1)
-        perm_s(0, 0)
         quantize_both(0, 0, 1)
+        perm_s(0, 0)
         b0 = [bank() for t in range(4)]
         for c in range(2):
             for t in range(4):
@@ -295,8 +304,8 @@ def tile_cachetocachegatedkeyfuser_x2_kernel(
         quantize_both(1, 0, 0)
         perm_w(1, 0, 0)
         perm_w(1, 0, 1)
-        perm_s(1, 0)
         quantize_both(1, 0, 1)
+        perm_s(1, 0)
         for x in range(2):
             perm_w(x, 1, 0)
             perm_w(x, 1, 1)
@@ -316,63 +325,99 @@ def tile_cachetocachegatedkeyfuser_x2_kernel(
                 for c in range(2):
                     s1_pass(b1, x, 0, 1, t, c)
             silu(0, 1, t, b1)
-            if t == 1:
-                for x in range(2):
-                    for tp in range(2):
-                        transposes(x, 1, tp)
-                        run(copy_q)
-                        quantize_both(x, 1, tp)
+            for x in {1:[0],2:[1]}.get(t, ()):
+                for tp in range(2):
+                    transposes(x, 1, tp)
+                    run(copy_q)
+                    quantize_both(x, 1, tp)
         hidden(0, 1)
 
-        for u in (0, 1, 8, 9, 2, 10, 3, 11, 4, 12, 5, 13, 6, 7, 14, 15, 16, 17, 18, 19, 20, 21, 22, 23):
-            if u < 8:
-                gf, t = divmod(u, 4)
+        for gf in range(2):
+            hq[1, gf] = keep.tile([P, 512], U32, name="hc1%d" % gf, align_bytes=256)
+            hs[1, gf] = keep.tile([P, 512], U8, name="hs1%d" % gf, align_bytes=256)
+
+        def slot_tt(gf, t, hh):
+            hbs = work.tile([P, 128, 4], BF16, name="hbs", align_bytes=256, bufs=3)
+            nc.vector.tensor_tensor(
+                out=hbs[:].rearrange("p (c i) t -> p c t i", i=4),
+                in0=hh[:].rearrange("p t (c i) -> p c t i", i=4),
+                in1=gt[:, gf, :].unsqueeze(1).unsqueeze(3).to_broadcast([P, 32, 4, 4]), op=ALU.mult)
+            qs_new.append((slot_q, (gf, t, hbs)))
+
+        def slot_q(gf, t, hbs):
+            n = slice(128 * t, 128 * (t + 1))
+            nc.vector.quantize_mx(out=hq[1, gf][:, n].bitcast(E4M3), scales=hs[1, gf][:, n],
+                                  in_=hbs[:].rearrange("p n t -> p (n t)"))
+
+        qs_new = []
+        units = ((1, 0, 0), (1, 0, 1), (2, 0, 0, 0), (2, 0, 0, 1), (1, 1, 0), (2, 0, 0, 2), (2, 0, 0, 3), (1, 1, 1), (2, 0, 1, 0), (2, 0, 1, 1), (1, 2, 0), (2, 0, 1, 2), (2, 0, 1, 3), (1, 2, 1), (2, 1, 0, 0), (2, 1, 1, 0), (1, 3, 0), (1, 3, 1), (2, 1, 0, 1), (2, 1, 1, 1), (2, 1, 0, 2), (2, 1, 0, 3), (2, 1, 1, 2), (2, 1, 1, 3))
+        for i, u in enumerate(units):
+            if u[0] == 1:
+                t, gf = u[1:]
                 b = bank()
-                for x in range(2):
-                    for c in range(2):
-                        s1_pass(b, x, 1, gf, t, c)
-                silu(1, gf, t, b)
+                b4 = b[:].rearrange("p (s n) -> p s n", s=4)
+                n = slice(128 * t, 128 * (t + 1))
+                for s in range(4):
+                    for x in range(2):
+                        for c in range(2):
+                            nc.tensor.matmul_mx(
+                                out=b4[:, s, :],
+                                lhsT=wp[x][:, c, gf, s, :].bitcast(E2M1), lhsT_scale=sp[x][:, c, gf, s, :],
+                                rhs=xc[x, 1, c][:, n].bitcast(E4M3), rhs_scale=xs[x, 1, c][:, n],
+                                start=(x == 0 and c == 0), stop=(x == 1 and c == 1),
+                            )
+                hh = work.tile([P, 4, 128], F32, name="hh", bufs=3)
+                nc.scalar.activation(out=hh[:].rearrange("p s n -> p (s n)"), in_=b[:], func=ACT.Silu)
                 run(dve_q, 2)
-                if (1, gf) in SPLIT:
-                    gain(1, gf, t)
-                    if t == 3:
-                        act_q = [(weave_q, (1, gf, k)) for k in range(4)] + act_q
-                elif t == 3:
-                    hidden(1, gf)
+                run(adds)
+                run(qs_new)
+                slot_tt(gf, t, hh)
             else:
-                g, nh, t = (u - 8) // 8, (u // 4) % 2, u % 4
-                if u == 16:
-                    run(act_q, 2)
-                if u >= 16 and u < 20 and (1, 1) in SPLIT:
-                    while (1, 1, t) not in woven:
-                        run(act_q, 1)
-                    run(dve_q)
-                if t == 0:
+                g, nh, t = u[1:]
+                if (g, nh) not in r:
                     r[g, nh] = work.tile([P, 4, 512], F32, name="r", bufs=3)
+                    done[g, nh] = 0
                 gate = s2_bank(g, t, nh, wg, sg)
                 delta = s2_bank(g, t, nh, wd, sd)
+                last = i == len(units) - 1
                 th = work.tile([P, 512], F32, name="th", bufs=4)
                 nc.scalar.activation(out=th[:], in_=gate[:], func=ACT.Tanh, scale=0.5)
                 run(dve_q, 2)
                 prod = work.tile([P, 512], F32, name="prod", bufs=4)
-                nc.vector.scalar_tensor_tensor(out=prod[:], in0=th[:], scalar=1.0, in1=delta[:], op0=ALU.add, op1=ALU.mult)
-                adds.append((s2_add, (g, nh, t, prod)))
-                if len(adds) > 1:
-                    run(adds, 1)
-            if copy_q:
-                run(copy_q, 2)
-                if not copy_q:
-                    quantize_both(1, 1, 0)
-                    quantize_both(1, 1, 1)
-            else:
+                if not last:
+                    nc.vector.scalar_tensor_tensor(out=prod[:], in0=th[:], scalar=1.0, in1=delta[:], op0=ALU.add, op1=ALU.mult)
+                    adds.append((s2_add, (g, nh, t, prod)))
+                    if qs_new and qs_new[0][1][0] == 1:
+                        run(qs_new)
+                    if len(adds) > 1:
+                        run(adds, 1)
+                    run(qs_new)
+                else:
+                    run(adds)
+                    for h in range(2):
+                        n = slice(256 * h, 256 * (h + 1))
+                        nc.vector.scalar_tensor_tensor(out=prod[:, n], in0=th[:, n], scalar=1.0, in1=delta[:, n], op0=ALU.add, op1=ALU.mult)
+                    for h in range(2):
+                        n = slice(256 * h, 256 * (h + 1))
+                        m = slice(512 * nh + 256 * h, 512 * nh + 256 * (h + 1))
+                        nc.vector.scalar_tensor_tensor(out=r[g, nh][:, t, n], in0=prod[:, n], scalar=0.5,
+                                                       in1=k_raw[0][g][:, t, m], op0=ALU.mult, op1=ALU.add)
+                    nc.sync.dma_start(out=o0[g, :, t, 512:1024], in_=r[g, nh][:, t, :])
+                    late.append((g, nh))
+            if act_q:
                 run(act_q, 1)
             if late and late[0] in ready:
                 act_q.extend((plane_cvt, late[0] + (k,)) for k in range(4))
                 late.pop(0)
             ready[:] = late
-        run(adds)
         for gn in late:
             act_q.extend((plane_cvt, gn + (k,)) for k in range(4))
-        while act_q:
-            run(act_q, 1)
-            run(dve_q)
+        on_act = [a for a in act_q if a[1] not in DVE_LAST]
+        on_dve = [a for a in act_q if a[1] in DVE_LAST]
+        act_q = []
+        run(on_dve, 2)
+        while on_act or on_dve:
+            run(on_act, 1)
+            run(on_dve, 1)
+            run(dve_q, 1)
+        run(dve_q)

@@ -63,10 +63,10 @@ def tile_cachetocachegatedkeyfuser_x2_kernel(
         def load_x(x, g, t0, t1):
             nc.sync.dma_start(out=k_raw[x][g][:, t0:t1, :], in_=k_hbm[x][g, :, t0:t1, :])
 
+        load_words(w_raw[0], w_recv_words, 0)
         load_x(0, 0, 0, 1)
         load_x(0, 0, 1, 2)
         load_x(0, 0, 2, 4)
-        load_words(w_raw[0], w_recv_words, 0)
         load_scales(s_raw[0], w_recv_scales, nc.scalar)
         load_x(1, 0, 0, 2)
         load_x(1, 0, 2, 4)
@@ -270,7 +270,7 @@ def tile_cachetocachegatedkeyfuser_x2_kernel(
             if k % 2 == 1:
                 dve_q.append((plane_q, (g, nh, k // 2)))
 
-        DVE_LAST = ((1, 1, 0), (1, 1, 1), (1, 1, 2), (1, 1, 3))
+        DVE_LAST = ((1, 1, 0), (1, 1, 1), (1, 1, 2))
 
         def plane_q(g, nh, k):
             rb, codes, scl = r[g, nh, 0]
@@ -285,18 +285,15 @@ def tile_cachetocachegatedkeyfuser_x2_kernel(
                     nc.sync.dma_start(out=out_2[g, 4 * q : 4 * q + 4, :].bitcast(I32),
                                       in_=out_scales[g][32 * q : 32 * q + 4, :].bitcast(I32))
 
-        for tp in range(2):
-            transposes(0, 0, tp)
-            run(copy_q)
-        transposes(1, 0, 0)
-        run(copy_q)
-        transposes(1, 0, 1)
-        run(copy_q)
-        quantize_both(0, 0, 0)
         perm_w(0, 0, 0)
         perm_w(0, 0, 1)
-        quantize_both(0, 0, 1)
+        for x in range(2):
+            for tp in range(2):
+                transposes(x, 0, tp)
+                run(copy_q)
+        quantize_both(0, 0, 0)
         perm_s(0, 0)
+        quantize_both(0, 0, 1)
         b0 = [bank() for t in range(4)]
         for c in range(2):
             for t in range(4):
@@ -304,8 +301,8 @@ def tile_cachetocachegatedkeyfuser_x2_kernel(
         quantize_both(1, 0, 0)
         perm_w(1, 0, 0)
         perm_w(1, 0, 1)
-        quantize_both(1, 0, 1)
         perm_s(1, 0)
+        quantize_both(1, 0, 1)
         for x in range(2):
             perm_w(x, 1, 0)
             perm_w(x, 1, 1)
@@ -325,7 +322,7 @@ def tile_cachetocachegatedkeyfuser_x2_kernel(
                 for c in range(2):
                     s1_pass(b1, x, 0, 1, t, c)
             silu(0, 1, t, b1)
-            for x in {1:[0],2:[1]}.get(t, ()):
+            for x in {1: [0], 2: [1]}.get(t, ()):
                 for tp in range(2):
                     transposes(x, 1, tp)
                     run(copy_q)
@@ -340,7 +337,7 @@ def tile_cachetocachegatedkeyfuser_x2_kernel(
             hbs = work.tile([P, 128, 4], BF16, name="hbs", align_bytes=256, bufs=3)
             nc.vector.tensor_tensor(
                 out=hbs[:].rearrange("p (c i) t -> p c t i", i=4),
-                in0=hh[:].rearrange("p t (c i) -> p c t i", i=4),
+                in0=hh.rearrange("p t (c i) -> p c t i", i=4),
                 in1=gt[:, gf, :].unsqueeze(1).unsqueeze(3).to_broadcast([P, 32, 4, 4]), op=ALU.mult)
             qs_new.append((slot_q, (gf, t, hbs)))
 
@@ -350,10 +347,25 @@ def tile_cachetocachegatedkeyfuser_x2_kernel(
                                   in_=hbs[:].rearrange("p n t -> p (n t)"))
 
         qs_new = []
-        units = ((1, 0, 0), (1, 0, 1), (2, 0, 0, 0), (2, 0, 0, 1), (1, 1, 0), (2, 0, 0, 2), (2, 0, 0, 3), (1, 1, 1), (2, 0, 1, 0), (2, 0, 1, 1), (1, 2, 0), (2, 0, 1, 2), (2, 0, 1, 3), (1, 2, 1), (2, 1, 0, 0), (2, 1, 1, 0), (1, 3, 0), (1, 3, 1), (2, 1, 0, 1), (2, 1, 1, 1), (2, 1, 0, 2), (2, 1, 0, 3), (2, 1, 1, 2), (2, 1, 1, 3))
+        wide = False
+        units = ((1, 0, 1), (1, 0, 0), (2, 0, 0, 0), (2, 0, 0, 1), (2, 0, 1, 0), (2, 0, 0, 2), (1, 1, 0), (2, 0, 0, 3), (2, 0, 1, 2), (1, 1, 1), (2, 0, 1, 1), (2, 0, 1, 3), (2, 1, 0, 0), (1, 2, 0), (2, 1, 1, 0), (1, 2, 1), (2, 1, 0, 1), (1, 3, 0), (1, 3, 1), (2, 1, 1, 1), (2, 1, 0, 2), (2, 1, 0, 3), (2, 1, 1, 2), (2, 1, 1, 3))
         for i, u in enumerate(units):
-            if u[0] == 1:
+            if u[0] == 3:
+                b = bank()
+                for x in range(2):
+                    for c in range(2):
+                        s1_pass(b, x, 1, 0, u[1], c)
+                if u[1] == 0:
+                    h32[1, 0] = work.tile([P, 4, 512], F32, name="h32", bufs=2)
+                nc.scalar.activation(out=h32[1, 0][:, u[1], :], in_=b[:], func=ACT.Silu)
+                run(dve_q, 2)
+                run(adds)
+                run(qs_new)
+            elif u[0] == 1:
                 t, gf = u[1:]
+                if gf == 1 and wide:
+                    slot_tt(0, t, h32[1, 0][:, :, 128 * t : 128 * (t + 1)])
+                    pass
                 b = bank()
                 b4 = b[:].rearrange("p (s n) -> p s n", s=4)
                 n = slice(128 * t, 128 * (t + 1))
@@ -371,7 +383,7 @@ def tile_cachetocachegatedkeyfuser_x2_kernel(
                 run(dve_q, 2)
                 run(adds)
                 run(qs_new)
-                slot_tt(gf, t, hh)
+                slot_tt(gf, t, hh[:])
             else:
                 g, nh, t = u[1:]
                 if (g, nh) not in r:

@@ -63,11 +63,11 @@ def tile_cachetocachegatedkeyfuser_x2_kernel(
         def load_x(x, g, t0, t1):
             nc.sync.dma_start(out=k_raw[x][g][:, t0:t1, :], in_=k_hbm[x][g, :, t0:t1, :])
 
-        load_words(w_raw[0], w_recv_words, 0)
         load_x(0, 0, 0, 1)
         load_x(0, 0, 1, 2)
         load_x(0, 0, 2, 4)
-        load_scales(s_raw[0], w_recv_scales, nc.scalar)
+        load_words(w_raw[0], w_recv_words, 0)
+        load_scales(s_raw[0], w_recv_scales, nc.sync)
         load_x(1, 0, 0, 2)
         load_x(1, 0, 2, 4)
         load_words(w_raw[1], w_share_words, 0)
@@ -285,15 +285,18 @@ def tile_cachetocachegatedkeyfuser_x2_kernel(
                     nc.sync.dma_start(out=out_2[g, 4 * q : 4 * q + 4, :].bitcast(I32),
                                       in_=out_scales[g][32 * q : 32 * q + 4, :].bitcast(I32))
 
+        for tp in range(2):
+            transposes(0, 0, tp)
+            run(copy_q)
+        transposes(1, 0, 0)
+        run(copy_q)
+        transposes(1, 0, 1)
+        run(copy_q)
+        quantize_both(0, 0, 0)
         perm_w(0, 0, 0)
         perm_w(0, 0, 1)
-        for x in range(2):
-            for tp in range(2):
-                transposes(x, 0, tp)
-                run(copy_q)
-        quantize_both(0, 0, 0)
-        perm_s(0, 0)
         quantize_both(0, 0, 1)
+        perm_s(0, 0)
         b0 = [bank() for t in range(4)]
         for c in range(2):
             for t in range(4):
@@ -301,8 +304,8 @@ def tile_cachetocachegatedkeyfuser_x2_kernel(
         quantize_both(1, 0, 0)
         perm_w(1, 0, 0)
         perm_w(1, 0, 1)
-        perm_s(1, 0)
         quantize_both(1, 0, 1)
+        perm_s(1, 0)
         for x in range(2):
             perm_w(x, 1, 0)
             perm_w(x, 1, 1)
@@ -322,7 +325,7 @@ def tile_cachetocachegatedkeyfuser_x2_kernel(
                 for c in range(2):
                     s1_pass(b1, x, 0, 1, t, c)
             silu(0, 1, t, b1)
-            for x in {1: [0], 2: [1]}.get(t, ()):
+            for x in {1:[0],2:[1]}.get(t, ()):
                 for tp in range(2):
                     transposes(x, 1, tp)
                     run(copy_q)
@@ -337,7 +340,7 @@ def tile_cachetocachegatedkeyfuser_x2_kernel(
             hbs = work.tile([P, 128, 4], BF16, name="hbs", align_bytes=256, bufs=3)
             nc.vector.tensor_tensor(
                 out=hbs[:].rearrange("p (c i) t -> p c t i", i=4),
-                in0=hh.rearrange("p t (c i) -> p c t i", i=4),
+                in0=hh[:].rearrange("p t (c i) -> p c t i", i=4),
                 in1=gt[:, gf, :].unsqueeze(1).unsqueeze(3).to_broadcast([P, 32, 4, 4]), op=ALU.mult)
             qs_new.append((slot_q, (gf, t, hbs)))
 
@@ -347,25 +350,10 @@ def tile_cachetocachegatedkeyfuser_x2_kernel(
                                   in_=hbs[:].rearrange("p n t -> p (n t)"))
 
         qs_new = []
-        wide = False
         units = ((1, 0, 1), (1, 0, 0), (2, 0, 0, 0), (2, 0, 0, 1), (2, 0, 1, 0), (2, 0, 0, 2), (1, 1, 0), (2, 0, 0, 3), (2, 0, 1, 2), (1, 1, 1), (2, 0, 1, 1), (2, 0, 1, 3), (2, 1, 0, 0), (1, 2, 0), (2, 1, 1, 0), (1, 2, 1), (2, 1, 0, 1), (1, 3, 0), (1, 3, 1), (2, 1, 1, 1), (2, 1, 0, 2), (2, 1, 0, 3), (2, 1, 1, 2), (2, 1, 1, 3))
         for i, u in enumerate(units):
-            if u[0] == 3:
-                b = bank()
-                for x in range(2):
-                    for c in range(2):
-                        s1_pass(b, x, 1, 0, u[1], c)
-                if u[1] == 0:
-                    h32[1, 0] = work.tile([P, 4, 512], F32, name="h32", bufs=2)
-                nc.scalar.activation(out=h32[1, 0][:, u[1], :], in_=b[:], func=ACT.Silu)
-                run(dve_q, 2)
-                run(adds)
-                run(qs_new)
-            elif u[0] == 1:
+            if u[0] == 1:
                 t, gf = u[1:]
-                if gf == 1 and wide:
-                    slot_tt(0, t, h32[1, 0][:, :, 128 * t : 128 * (t + 1)])
-                    pass
                 b = bank()
                 b4 = b[:].rearrange("p (s n) -> p s n", s=4)
                 n = slice(128 * t, 128 * (t + 1))
@@ -383,7 +371,7 @@ def tile_cachetocachegatedkeyfuser_x2_kernel(
                 run(dve_q, 2)
                 run(adds)
                 run(qs_new)
-                slot_tt(gf, t, hh[:])
+                slot_tt(gf, t, hh)
             else:
                 g, nh, t = u[1:]
                 if (g, nh) not in r:

from contextlib import ExitStack

import concourse.mybir as mybir
from concourse.masks import make_identity

F32 = mybir.dt.float32
BF16 = mybir.dt.bfloat16
U32 = mybir.dt.uint32
I32 = mybir.dt.int32
U8 = mybir.dt.uint8
E4M3 = mybir.dt.float8_e4m3fn_x4
E2M1 = mybir.dt.float4_e2m1fn_x4
ACT = mybir.ActivationFunctionType
ALU = mybir.AluOpType

P = 128
T = D = F = 1024
FLOPS = 4 * 2 * T * D * F


def tile_cachetocachegatedkeyfuser_x2_kernel(
    tc, k_recv, k_share, w_recv_words, w_recv_scales, w_share_words, w_share_scales,
    g_hid, w_delta_words, w_delta_scales, w_gate_words, w_gate_scales, out_0, out_1, out_2,
):
    nc = tc.nc
    with ExitStack() as ctx:
        keep = ctx.enter_context(tc.tile_pool(name="keep", bufs=1))
        work = ctx.enter_context(tc.tile_pool(name="work", bufs=3))
        psum = ctx.enter_context(tc.psum_pool(name="psum", bufs=8))
        ctx.enter_context(tc.manual_schedule())


        warm = keep.tile([P, 1], F32, name="warm")
        nc.vector.memset(warm[:], 0.0)
        nc.scalar.activation(out=warm[:], in_=warm[:], func=ACT.Silu)

        def plane(name):
            return (keep.tile([P, 2, 2048], U8, name=name + "_w", align_bytes=256),
                    keep.tile([P, 2, 1024], U8, name=name + "_s", align_bytes=256))

        w_raw, s_raw = zip(plane("recv"), plane("share"))
        wd, sd = plane("delta")
        wg, sg = plane("gate")
        for s in (s_raw[0], s_raw[1], sd, sg):
            nc.vector.memset(s[:].rearrange("p g n -> p (g n)").bitcast(I32), 0)
        ident = keep.tile([P, P], F32, name="ident")
        make_identity(nc, ident[:])

        k_raw = [[keep.tile([P, 4, 1024], BF16, name="k%d%d" % (x, g), align_bytes=256) for g in range(2)] for x in range(2)]
        k_hbm = [k.rearrange("(g p t) d -> g p t d", g=2, t=4) for k in (k_recv, k_share)]

        def load_words(tile, hbm, gf=None):
            b = slice(0, 2048) if gf is None else slice(1024 * gf, 1024 * (gf + 1))
            nc.sync.dma_start(out=tile[:, :, b].bitcast(I32), in_=hbm[:, :, b].rearrange("g p n -> p g n").bitcast(I32))

        def load_scales(tile, hbm, engine):
            for q in range(4):
                engine.dma_start(
                    out=tile[32 * q : 32 * q + 4, :, :].bitcast(I32),
                    in_=hbm[:, 4 * q : 4 * q + 4, :].rearrange("g r n -> r g n").bitcast(I32),
                )

        def load_x(x, g, t0, t1):
            nc.sync.dma_start(out=k_raw[x][g][:, t0:t1, :], in_=k_hbm[x][g, :, t0:t1, :])

        load_x(0, 0, 0, 1)
        load_x(0, 0, 1, 2)
        load_x(0, 0, 2, 4)
        load_words(w_raw[0], w_recv_words, 0)
        load_scales(s_raw[0], w_recv_scales, nc.sync)
        load_x(1, 0, 0, 2)
        load_x(1, 0, 2, 4)
        load_words(w_raw[1], w_share_words, 0)
        load_scales(s_raw[1], w_share_scales, nc.sync)
        load_words(w_raw[0], w_recv_words, 1)
        load_words(w_raw[1], w_share_words, 1)
        gt = keep.tile([P, 2, 4], BF16, name="gt")
        nc.sync.dma_start(out=gt[:], in_=g_hid.rearrange("(g p t) -> p g t", g=2, t=4))
        load_x(0, 1, 0, 4)
        load_x(1, 1, 0, 4)
        load_scales(sd, w_delta_scales, nc.sync)
        load_scales(sg, w_gate_scales, nc.sync)
        load_words(wd, w_delta_words)
        load_words(wg, w_gate_words)

        wp = [keep.tile([P, 2, 2, 4, 256], U8, name="wp%d" % x, align_bytes=256) for x in range(2)]
        sp = [keep.tile([P, 2, 2, 4, 128], U8, name="sp%d" % x, align_bytes=256) for x in range(2)]

        def perm_w(x, gf, c):
            nc.vector.tensor_copy(
                out=wp[x][:, c, gf, :, :].rearrange("p t (m b) -> p t m b", b=2),
                in_=w_raw[x][:, c, 1024 * gf : 1024 * (gf + 1)].rearrange("p (m t b) -> p t m b", t=4, b=2),
            )

        def perm_s(x, gf):
            nc.vector.tensor_copy(
                out=sp[x][:, :, gf, :, :],
                in_=s_raw[x][:, :, 512 * gf : 512 * (gf + 1)].rearrange("p c (m t) -> p c t m", t=4),
            )

        xc = {}
        xs = {}
        grp = {}
        for x in range(2):
            for g in range(2):
                for c in range(2):
                    xc[x, g, c] = keep.tile([P, 512], U32, name="xc%d%d%d" % (x, g, c), align_bytes=256)
                    xs[x, g, c] = keep.tile([P, 512], U8, name="xs%d%d%d" % (x, g, c), align_bytes=256)

        def bank():
            return psum.tile([P, 512], F32, name="ps")

        k_words = {}
        DEINT = ((0, 1), (1, 1))

        def deinterleave(x, g, tp):
            if tp == 0:
                k_words[x, g] = keep.tile([P, 4, 2, 2, 128], F32, name="kw%d%d" % (x, g), align_bytes=256)
            t = slice(2 * tp, 2 * tp + 2)
            nc.vector.tensor_copy(out=k_words[x, g][:, t].rearrange("p t c u w -> p (t c) u w"),
                           in_=k_raw[x][g][:, t, :].bitcast(F32).rearrange("p t (c w u) -> p (t c) u w", c=2, u=2))

        def transposes(x, g, tp):
            for c in range(2):
                if tp == 0:
                    grp[x, g, c] = work.tile([P, 512, 4], BF16, name="grp%d" % c, align_bytes=256, bufs=3)
                xt = bank()
                xt4 = xt[:].rearrange("p (a u r) -> p a u r", a=2, u=2)
                for tt in range(2):
                    for u in range(2):
                        if (x, g) in DEINT:
                            words = k_words[x, g][:, 2 * tp + tt, c, u, :]
                        else:
                            words = k_raw[x][g][:, 2 * tp + tt, :].bitcast(F32)[:, 256 * c + u : 256 * (c + 1) : 2]
                        nc.tensor.transpose(xt4[:, tt, u, :], words, ident[:])
                copy_q.append((copy_out, (x, g, c, tp, xt4)))

        def copy_out(x, g, c, tp, xt4):
            dst = grp[x, g, c][:, 256 * tp : 256 * (tp + 1), :].bitcast(F32).rearrange("p (a r) u -> p a r u", a=2)
            nc.scalar.copy(out=dst, in_=xt4.rearrange("p a u r -> p a r u"))

        copy_q = []
        act_q = []
        dve_q = []
        tt_q = []

        def run(q, n=99):
            for i in range(n):
                if q:
                    f, a = q.pop(0)
                    f(*a)

        def quantize_x(x, g, c, tp):
            n = slice(256 * tp, 256 * (tp + 1))
            nc.vector.quantize_mx(out=xc[x, g, c][:, n].bitcast(E4M3), scales=xs[x, g, c][:, n],
                                  in_=grp[x, g, c][:, n, :].rearrange("p n t -> p (n t)"))

        def quantize_both(x, g, tp):
            quantize_x(x, g, 0, tp)
            quantize_x(x, g, 1, tp)

        def s1_pass(b, x, g, gf, t, c):
            nc.tensor.matmul_mx(
                out=b[:],
                lhsT=wp[x][:, c, gf, t, :].bitcast(E2M1), lhsT_scale=sp[x][:, c, gf, t, :],
                rhs=xc[x, g, c][:].bitcast(E4M3), rhs_scale=xs[x, g, c][:],
                start=(x == 0 and c == 0), stop=(x == 1 and c == 1),
            )

        hq = {}
        hs = {}
        h32 = {}
        ht = {}
        SPLIT = ()

        hb = {}

        def silu(g, gf, t, b):
            if t == 0:
                h32[g, gf] = work.tile([P, 4, 512], F32, name="h32", bufs=2)
                hb[g, gf] = work.tile([P, 512, 4], BF16, name="hb", align_bytes=256, bufs=2)
                hq[g, gf] = keep.tile([P, 512], U32, name="hc%d%d" % (g, gf), align_bytes=256)
                hs[g, gf] = keep.tile([P, 512], U8, name="hs%d%d" % (g, gf), align_bytes=256)
                if (g, gf) in SPLIT:
                    ht[g, gf] = work.tile([P, 4, 512], BF16, name="ht", align_bytes=256, bufs=2)
            nc.scalar.activation(out=h32[g, gf][:, t, :], in_=b[:], func=ACT.Silu)

        def gain(g, gf, t):
            nc.vector.tensor_scalar(out=ht[g, gf][:, t, :], in0=h32[g, gf][:, t, :], scalar1=gt[:, gf, t : t + 1],
                                    scalar2=None, op0=ALU.mult)

        def weave(g, gf, k):
            c = slice(32 * k, 32 * (k + 1))
            nc.scalar.copy(out=hb[g, gf][:].rearrange("p (c i) t -> p c t i", i=4)[:, c],
                           in_=ht[g, gf][:].rearrange("p t (c i) -> p c t i", i=4)[:, c])

        woven = []

        def weave_q(g, gf, k):
            weave(g, gf, k)
            woven.append((g, gf, k))
            dve_q.append((hidden_q, (g, gf, k)))

        def hidden_tt(g, gf, k):
            c = slice(32 * k, 32 * (k + 1))
            nc.vector.tensor_tensor(
                out=hb[g, gf][:].rearrange("p (c i) t -> p c t i", i=4)[:, c],
                in0=h32[g, gf][:].rearrange("p t (c i) -> p c t i", i=4)[:, c],
                in1=gt[:, gf, :].unsqueeze(1).unsqueeze(3).to_broadcast([P, 32, 4, 4]), op=ALU.mult)

        def hidden_q(g, gf, k):
            n = slice(128 * k, 128 * (k + 1))
            nc.vector.quantize_mx(out=hq[g, gf][:, n].bitcast(E4M3), scales=hs[g, gf][:, n],
                                  in_=hb[g, gf][:, n, :].rearrange("p n t -> p (n t)"))

        def hidden(g, gf):
            hidden_tt(g, gf, 0)
            for k in range(1, 4):
                hidden_tt(g, gf, k)
                hidden_q(g, gf, k - 1)
            hidden_q(g, gf, 3)

        o0 = out_0.rearrange("(g p t) d -> g p t d", g=2, t=4)

        def s2_bank(g, t, nh, w, s):
            b = bank()
            for gf in range(2):
                nc.tensor.matmul_mx(
                    out=b[:],
                    lhsT=hq[g, gf][:, 128 * t : 128 * (t + 1)].bitcast(E4M3),
                    lhsT_scale=hs[g, gf][:, 128 * t : 128 * (t + 1)],
                    rhs=w[:, gf, 1024 * nh : 1024 * (nh + 1)].bitcast(E2M1),
                    rhs_scale=s[:, gf, 512 * nh : 512 * (nh + 1)],
                    start=(gf == 0), stop=(gf == 1),
                )
            return b

        r = {}

        adds = []
        done = {}
        late = []
        ready = []

        def s2_add(g, nh, t, prod):
            cols = slice(512 * nh, 512 * (nh + 1))
            nc.vector.scalar_tensor_tensor(out=r[g, nh][:, t, :], in0=prod[:], scalar=0.5,
                                           in1=k_raw[0][g][:, t, cols], op0=ALU.mult, op1=ALU.add)
            nc.sync.dma_start(out=o0[g, :, t, cols], in_=r[g, nh][:, t, :])
            done[g, nh] += 1
            if done[g, nh] == 4:
                late.append((g, nh))

        out_scales = [keep.tile([P, 1024], U8, name="os%d" % g, align_bytes=256) for g in range(2)]
        stored = [0, 0]

        def plane_cvt(g, nh, k):
            if k == 0:
                r[g, nh, 0] = (work.tile([P, 512, 4], BF16, name="rb", align_bytes=256, bufs=2),
                               work.tile([P, 512], U32, name="oc", align_bytes=256, bufs=2),
                               out_scales[g][:, 512 * nh : 512 * (nh + 1)])
            rb = r[g, nh, 0][0]
            c = slice(32 * k, 32 * (k + 1))
            dst = rb[:].rearrange("p (c i) t -> p c t i", i=4)[:, c]
            src = r[g, nh][:].rearrange("p t (c i) -> p c t i", i=4)[:, c]
            if (g, nh, k) in DVE_LAST:
                nc.vector.tensor_copy(out=dst, in_=src)
            else:
                nc.scalar.copy(out=dst, in_=src)
            if k % 2 == 1:
                dve_q.append((plane_q, (g, nh, k // 2)))

        DVE_LAST = ((1, 1, 0), (1, 1, 1), (1, 1, 2))

        def plane_q(g, nh, k):
            rb, codes, scl = r[g, nh, 0]
            m = slice(256 * k, 256 * (k + 1))
            nc.vector.quantize_mx(out=codes[:, m].bitcast(E4M3), scales=scl[:, m],
                                  in_=rb[:, m, :].rearrange("p m t -> p (m t)"))
            c = slice(512 * nh + 256 * k, 512 * nh + 256 * (k + 1))
            nc.sync.dma_start(out=out_1[g, :, c, :].rearrange("p m t -> p (m t)").bitcast(I32), in_=codes[:, m].bitcast(I32))
            stored[g] += 1
            if stored[g] == 4:
                for q in range(4):
                    nc.sync.dma_start(out=out_2[g, 4 * q : 4 * q + 4, :].bitcast(I32),
                                      in_=out_scales[g][32 * q : 32 * q + 4, :].bitcast(I32))

        for tp in range(2):
            transposes(0, 0, tp)
            run(copy_q)
        transposes(1, 0, 0)
        run(copy_q)
        transposes(1, 0, 1)
        run(copy_q)
        quantize_both(0, 0, 0)
        perm_w(0, 0, 0)
        perm_w(0, 0, 1)
        quantize_both(0, 0, 1)
        perm_s(0, 0)
        b0 = [bank() for t in range(4)]
        for c in range(2):
            for t in range(4):
                s1_pass(b0[t], 0, 0, 0, t, c)
        quantize_both(1, 0, 0)
        perm_w(1, 0, 0)
        perm_w(1, 0, 1)
        quantize_both(1, 0, 1)
        perm_s(1, 0)
        for x in range(2):
            perm_w(x, 1, 0)
            perm_w(x, 1, 1)
            perm_s(x, 1)
        for t in range(4):
            for c in range(2):
                s1_pass(b0[t], 1, 0, 0, t, c)
            silu(0, 0, t, b0[t])
        for x in range(2):
            if (x, 1) in DEINT:
                deinterleave(x, 1, 0)
                deinterleave(x, 1, 1)
        hidden(0, 0)
        for t in range(4):
            b1 = bank()
            for x in range(2):
                for c in range(2):
                    s1_pass(b1, x, 0, 1, t, c)
            silu(0, 1, t, b1)
            for x in {1:[0],2:[1]}.get(t, ()):
                for tp in range(2):
                    transposes(x, 1, tp)
                    run(copy_q)
                    quantize_both(x, 1, tp)
        hidden(0, 1)

        for gf in range(2):
            hq[1, gf] = keep.tile([P, 512], U32, name="hc1%d" % gf, align_bytes=256)
            hs[1, gf] = keep.tile([P, 512], U8, name="hs1%d" % gf, align_bytes=256)

        def slot_tt(gf, t, hh):
            hbs = work.tile([P, 128, 4], BF16, name="hbs", align_bytes=256, bufs=3)
            nc.vector.tensor_tensor(
                out=hbs[:].rearrange("p (c i) t -> p c t i", i=4),
                in0=hh[:].rearrange("p t (c i) -> p c t i", i=4),
                in1=gt[:, gf, :].unsqueeze(1).unsqueeze(3).to_broadcast([P, 32, 4, 4]), op=ALU.mult)
            qs_new.append((slot_q, (gf, t, hbs)))

        def slot_q(gf, t, hbs):
            n = slice(128 * t, 128 * (t + 1))
            nc.vector.quantize_mx(out=hq[1, gf][:, n].bitcast(E4M3), scales=hs[1, gf][:, n],
                                  in_=hbs[:].rearrange("p n t -> p (n t)"))

        qs_new = []
        units = ((1, 0, 1), (1, 0, 0), (2, 0, 0, 0), (2, 0, 0, 1), (2, 0, 1, 0), (2, 0, 0, 2), (1, 1, 0), (2, 0, 0, 3), (2, 0, 1, 2), (1, 1, 1), (2, 0, 1, 1), (2, 0, 1, 3), (2, 1, 0, 0), (1, 2, 0), (2, 1, 1, 0), (1, 2, 1), (2, 1, 0, 1), (1, 3, 0), (1, 3, 1), (2, 1, 1, 1), (2, 1, 0, 2), (2, 1, 0, 3), (2, 1, 1, 2), (2, 1, 1, 3))
        for i, u in enumerate(units):
            if u[0] == 1:
                t, gf = u[1:]
                b = bank()
                b4 = b[:].rearrange("p (s n) -> p s n", s=4)
                n = slice(128 * t, 128 * (t + 1))
                for s in range(4):
                    for x in range(2):
                        for c in range(2):
                            nc.tensor.matmul_mx(
                                out=b4[:, s, :],
                                lhsT=wp[x][:, c, gf, s, :].bitcast(E2M1), lhsT_scale=sp[x][:, c, gf, s, :],
                                rhs=xc[x, 1, c][:, n].bitcast(E4M3), rhs_scale=xs[x, 1, c][:, n],
                                start=(x == 0 and c == 0), stop=(x == 1 and c == 1),
                            )
                hh = work.tile([P, 4, 128], F32, name="hh", bufs=3)
                nc.scalar.activation(out=hh[:].rearrange("p s n -> p (s n)"), in_=b[:], func=ACT.Silu)
                run(dve_q, 2)
                run(adds)
                run(qs_new)
                slot_tt(gf, t, hh)
            else:
                g, nh, t = u[1:]
                if (g, nh) not in r:
                    r[g, nh] = work.tile([P, 4, 512], F32, name="r", bufs=3)
                    done[g, nh] = 0
                gate = s2_bank(g, t, nh, wg, sg)
                delta = s2_bank(g, t, nh, wd, sd)
                last = i == len(units) - 1
                th = work.tile([P, 512], F32, name="th", bufs=4)
                nc.scalar.activation(out=th[:], in_=gate[:], func=ACT.Tanh, scale=0.5)
                run(dve_q, 2)
                prod = work.tile([P, 512], F32, name="prod", bufs=4)
                if not last:
                    nc.vector.scalar_tensor_tensor(out=prod[:], in0=th[:], scalar=1.0, in1=delta[:], op0=ALU.add, op1=ALU.mult)
                    adds.append((s2_add, (g, nh, t, prod)))
                    if qs_new and qs_new[0][1][0] == 1:
                        run(qs_new)
                    if len(adds) > 1:
                        run(adds, 1)
                    run(qs_new)
                else:
                    run(adds)
                    for h in range(2):
                        n = slice(256 * h, 256 * (h + 1))
                        nc.vector.scalar_tensor_tensor(out=prod[:, n], in0=th[:, n], scalar=1.0, in1=delta[:, n], op0=ALU.add, op1=ALU.mult)
                    for h in range(2):
                        n = slice(256 * h, 256 * (h + 1))
                        m = slice(512 * nh + 256 * h, 512 * nh + 256 * (h + 1))
                        nc.vector.scalar_tensor_tensor(out=r[g, nh][:, t, n], in0=prod[:, n], scalar=0.5,
                                                       in1=k_raw[0][g][:, t, m], op0=ALU.mult, op1=ALU.add)
                    nc.sync.dma_start(out=o0[g, :, t, 512:1024], in_=r[g, nh][:, t, :])
                    late.append((g, nh))
            if act_q:
                run(act_q, 1)
            if late and late[0] in ready:
                act_q.extend((plane_cvt, late[0] + (k,)) for k in range(4))
                late.pop(0)
            ready[:] = late
        for gn in late:
            act_q.extend((plane_cvt, gn + (k,)) for k in range(4))
        on_act = [a for a in act_q if a[1] not in DVE_LAST]
        on_dve = [a for a in act_q if a[1] in DVE_LAST]
        act_q = []
        run(on_dve, 2)
        while on_act or on_dve:
            run(on_act, 1)
            run(on_dve, 1)
            run(dve_q, 1)
        run(dve_q)
